import numpy as np
import ml_dtypes


def mxq(x, axis, fmt="e4m3"):
    dtype, down = {"e4m3": (ml_dtypes.float8_e4m3fn, 7), "e5m2": (ml_dtypes.float8_e5m2, 14)}[fmt]
    v = np.moveaxis(np.asarray(x, np.float32).astype(ml_dtypes.bfloat16).astype(np.float64), axis, -1)
    blocks = v.reshape(v.shape[:-1] + (-1, 32))
    amax = np.abs(blocks).max(-1, keepdims=True)
    byte = np.maximum(np.where(amax > 0, np.frexp(amax)[1] - 1 + 127, 0) - down, 1)
    scale = np.exp2(byte - 127.0)
    codes = (blocks / scale).astype(np.float32).astype(dtype).astype(np.float64)
    return np.moveaxis((codes * scale).reshape(v.shape), -1, axis)


WIDE = False


def mx_kscale(k):
    if not WIDE:
        return np.ones(k)
    levels = np.array([10, -10, 5, -5, 0])
    if k % 512:
        return np.exp2(np.random.permutation(np.resize(levels, k // 32))).repeat(32)
    a = np.empty((k // 512, 16))
    for p in range(k // 512):
        a[p, :8] = np.random.permutation(np.resize(levels, 8))
        for g in range(8):
            far = levels[np.abs(levels - a[p, g]) >= 10]
            a[p, g + 8] = far[np.random.randint(len(far))]
    return np.exp2(a.ravel()).repeat(32)


def f64(x):
    return np.asarray(x).astype(np.float64)


def striped(idx):
    return np.tile(np.asarray(idx).reshape(-1, 16).T, (8, 1)).astype(np.uint16)


def unstriped(offs):
    return offs[:16].T.reshape(-1).astype(np.int64)


E2M1 = np.array([0.0, 0.5, 1.0, 1.5, 2.0, 3.0, 4.0, 6.0, -0.0, -0.5, -1.0, -1.5, -2.0, -3.0, -4.0, -6.0])


def pack_weight(w, fmt):
    k, n = w.shape
    w = f64(np.asarray(w, np.float32).astype(ml_dtypes.bfloat16)).reshape(k // 32, 32, n)
    amax = np.abs(w).max(1)
    if fmt == "e4m3":
        byte = np.frexp(amax)[1] - 1 + 127 - 7
    else:
        mant, ex = np.frexp(amax / 6.0)
        byte = np.where(mant > 0.5, ex, ex - 1) + 127
    byte = np.clip(np.where(amax > 0, byte, 1), 1, 254)
    scaled = (w * np.exp2(127.0 - byte)[:, None, :]).reshape(k, n).astype(np.float32)
    by_word = np.ascontiguousarray(scaled.reshape(k // 512, 128, 4, n).transpose(0, 1, 3, 2))
    if fmt == "e4m3":
        words = by_word.astype(ml_dtypes.float8_e4m3fn).view(np.uint8)
    else:
        c = by_word.astype(ml_dtypes.float4_e2m1fn).view(np.uint8) & 0xF
        words = (c[..., 0::2] | (c[..., 1::2] << 4)).reshape(k // 512, 128, 2 * n)
    return np.ascontiguousarray(words), np.ascontiguousarray(byte.astype(np.uint8).reshape(k // 512, 16, n))


def unpack_weight(words, scales, fmt):
    g, _, n = scales.shape
    words = np.ascontiguousarray(words).reshape(g, 128, n, -1)
    if fmt == "e4m3":
        vals = words.view(ml_dtypes.float8_e4m3fn).astype(np.float64)
    else:
        nib = np.empty((g, 128, n, 4), np.uint8)
        nib[..., 0::2] = words & 0xF
        nib[..., 1::2] = words >> 4
        vals = E2M1[nib]
    vals = vals * np.repeat(np.exp2(scales.astype(np.float64) - 127.0), 8, axis=1)[..., None]
    return vals.transpose(0, 1, 3, 2).reshape(g * 512, n)


def sigmoid(v):
    return 1.0 / (1.0 + np.exp(-v))


def bf(x):
    return np.asarray(x, np.float32).astype(ml_dtypes.bfloat16)


def planes(Y):
    r, m = Y.shape
    b = f64(bf(Y)).reshape(r // 32, 32, m)
    amax = np.abs(b).max(1)
    byte = np.clip(np.where(amax > 0, np.frexp(amax)[1] - 1 + 127 - 7, 1), 1, 254)
    codes = (b * np.exp2(127.0 - byte)[:, None, :]).reshape(r, m).astype(np.float32).astype(ml_dtypes.float8_e4m3fn).view(np.uint8)
    words = codes.reshape(r // 512, 128, 4, m).transpose(0, 1, 3, 2)
    return np.ascontiguousarray(words), np.ascontiguousarray(byte.astype(np.uint8).reshape(r // 512, 16, m))


D, E, T, I, Q, G = 512, 512, 2048, 512, 256, 32


def setup_inputs():
    n = np.random.standard_normal
    idx = np.random.permutation(T)[:I]
    fd = mx_kscale(D)
    fi = mx_kscale(I)
    ti = np.ones(T)
    ti[idx] = fi
    keysp = pack_weight(n((D, T)) / fd[:, None], "e2m1")
    return {
        "query": (n((D, Q)) * 0.5 / np.sqrt(D) * fd[:, None]).astype(np.float32),
        "keys_words": keysp[0],
        "keys_scales": keysp[1],
        "helpf": (np.random.uniform(0.5, 1.5, (Q, 1))).astype(np.float32),
        "os": (np.random.uniform(4.0, 16.0, (1, I)) * fi).astype(np.float32),
        "vals": (n((E, T)) / ti).astype(np.float32),
        "offs": striped(idx),
    }


def reference(query, keys_words, keys_scales, helpf, os, vals, offs):
    idx = unstriped(offs)
    keysu = unpack_weight(keys_words, keys_scales, "e2m1")
    queryq = mxq(f64(query), 0, "e4m3")
    keysidxg = keysu[:, idx]
    a = queryq.T @ keysidxg
    m1 = a.reshape(Q, G, I // G).mean(axis=2)
    gt = sigmoid(m1 * 4.0)
    gr = np.repeat(gt, I // G, axis=1)
    s = a * (gr * f64(helpf) + 1.0)
    p = np.exp(s - np.max(s, axis=1, keepdims=True))
    z = np.sum(p, axis=1, keepdims=True)
    w = p / z
    wo1 = w * f64(os)
    wt1 = wo1.T
    vt1 = f64(vals)[:, idx].T
    vt1q = mxq(vt1, 0, "e4m3")
    wt1q = mxq(wt1, 0, "e4m3")
    o = vt1q.T @ wt1q
    words, scales = planes(o)
    return o, words, scales

@@ -1,0 +1,240 @@
+from contextlib import ExitStack
+
+import concourse.mybir as mybir
+
+D, E, T, SLOTS, Q, PAGES = 512, 512, 2048, 512, 256, 32
+PAGE = SLOTS // PAGES
+P = 128
+PACK = 4
+HALVES = Q // P
+
+FLOPS = 2 * D * Q * SLOTS + 2 * SLOTS * E * Q
+
+F32 = mybir.dt.float32
+BF16 = mybir.dt.bfloat16
+I32 = mybir.dt.int32
+U32 = mybir.dt.uint32
+U16 = mybir.dt.uint16
+U8 = mybir.dt.uint8
+FP8X4 = mybir.dt.float8_e4m3fn_x4
+FP4X4 = mybir.dt.float4_e2m1fn_x4
+ALU = mybir.AluOpType
+ACT = mybir.ActivationFunctionType
+AXIS = mybir.AxisListType
+
+
+def tile_attend_pagemates_pl_kernel(
+    tc, query, keys_words, keys_scales, helpf, slot_factor, vals, offs, out_0, out_1, out_2
+):
+    nc = tc.nc
+    with ExitStack() as ctx:
+        sb = ctx.enter_context(tc.tile_pool(name="sb", bufs=1))
+        ps = ctx.enter_context(tc.psum_pool(name="ps", bufs=1))
+
+        def tile(shape, dtype, name, tag=None):
+            return sb.tile(shape, dtype, align_bytes=64, name=name, tag=tag or name)
+
+        halves = range(HALVES)
+        cols = [slice(h * P, (h + 1) * P) for h in halves]
+
+        key_scale_pool = tile([P, T], U8, "key_scale_pool", "buffer3")
+        nc.vector.memset(key_scale_pool[:].bitcast(I32), 0)
+        zeros = tile([P, P], F32, "zeros", "columns")
+        nc.vector.memset(zeros[:], 0.0)
+        identity = tile([P, P], F32, "identity")
+        nc.gpsimd.affine_select(
+            out=identity[:],
+            in_=zeros[:],
+            compare_op=ALU.not_equal,
+            fill=1.0,
+            base=0,
+            pattern=[[-1, P]],
+            channel_multiplier=1,
+        )
+
+        offsets = sb.tile([P, SLOTS // 16], U16)
+        nc.sync.dma_start(offsets[:], offs)
+        help_cols = tile([P, HALVES], F32, "help_cols", "buffer0")
+        with nc.allow_non_contiguous_dma(reason="one help value a partition for each half of the query rows"):
+            nc.sync.dma_start(help_cols[:], helpf.rearrange("(h p) o -> p (h o)", p=P))
+        key_word_pool = tile([P, T], U16, "key_word_pool", "buffer1")
+        nc.sync.dma_start(key_word_pool[:].bitcast(I32), keys_words[0].bitcast(I32))
+        query_raw = tile([P, PACK, Q], F32, "query_raw", "buffer2")
+        nc.sync.dma_start(query_raw[:], query.rearrange("(p j) q -> p j q", j=PACK))
+        for quad in range(4):
+            nc.scalar.dma_start(
+                key_scale_pool[32 * quad : 32 * quad + 4, :].bitcast(I32),
+                keys_scales[0][4 * quad : 4 * quad + 4, :].bitcast(I32),
+            )
+
+        half_help = tile([P, HALVES], F32, "half_help")
+        nc.vector.tensor_scalar(half_help[:], help_cols[:], 0.5, None, ALU.mult)
+        half_help_1 = tile([P, HALVES], F32, "half_help_1")
+        nc.vector.tensor_scalar(half_help_1[:], help_cols[:], 0.5, 1.0, ALU.mult, ALU.add)
+
+        key_words = tile([P, SLOTS], U16, "key_words")
+        nc.vector.tensor_copy(key_words[:], key_word_pool[:].indirect(offsets[:]))
+        key_scales = tile([P, SLOTS], U8, "key_scales")
+        nc.vector.tensor_copy(key_scales[:], key_scale_pool[:].indirect(offsets[:]))
+
+        def quantize(grouped, codes, scales):
+            nc.vector.quantize_mx(out=codes.bitcast(FP8X4), scales=scales, in_=grouped)
+
+        query_codes = tile([P, Q], U32, "query_codes", "buffer3")
+        query_scales = tile([P, Q], U8, "query_scales")
+        for h in halves:
+            query_bf = tile([P, P, PACK], BF16, "query_bf%d" % h, "picked0" if h == 0 else None)
+            nc.scalar.activation(query_bf[:], query_raw[:, :, cols[h]].rearrange("p j q -> p q j"), ACT.Copy)
+            quantize(query_bf[:].rearrange("p q j -> p (q j)"), query_codes[:, cols[h]], query_scales[:, cols[h]])
+
+        val_rows = vals.rearrange("(p t) c -> t p c", t=PACK)
+
+        def load_values(t):
+            val_pool = tile([P, T], F32, "val_pool%d" % t, "buffer%d" % t)
+            nc.sync.dma_start(val_pool[:], val_rows[t])
+            return val_pool
+
+        val_pools = [load_values(0)]
+        factor_cols = tile([P, PACK], F32, "factor_cols", "columns")
+        nc.sync.dma_start(factor_cols[:], slot_factor.rearrange("o (s r) -> s (o r)", r=PACK))
+        val_pools.extend([load_values(1), load_values(2)])
+
+        scores = [ps.tile([P, PAGES, PAGE], F32, name="scores%d" % h) for h in halves]
+        for h in halves:
+            nc.tensor.matmul_mx(
+                out=scores[h][:].rearrange("p g k -> p (g k)"),
+                lhsT=query_codes[:, cols[h]].bitcast(FP8X4),
+                lhsT_scale=query_scales[:, cols[h]],
+                rhs=key_words[:].bitcast(FP4X4),
+                rhs_scale=key_scales[:],
+                start=True,
+                stop=True,
+            )
+        val_pools.append(load_values(3))
+
+        def turn_slots(rows_bf, name, bank):
+            words = rows_bf[:].bitcast(F32)
+            turned = ps.tile([P, 2, P], F32, name=name + "_turned", tag=bank)
+            for u in range(2):
+                nc.tensor.transpose(turned[:, u, :], words[:, u : SLOTS // 2 : 2], identity[:])
+            grouped = tile([P, P * PACK], BF16, name + "_grouped")
+            nc.scalar.copy(
+                grouped[:].bitcast(F32).rearrange("p (c u) -> p c u", u=2),
+                turned[:].rearrange("p u c -> p c u"),
+            )
+            return grouped
+
+        def pick_values(t, bank):
+            picked = tile([P, SLOTS], BF16, "picked%d" % t)
+            nc.vector.tensor_copy(picked[:], val_pools[t][:].indirect(offsets[:]))
+            return turn_slots(picked, "val%d" % t, bank)
+
+        def quantize_values(t, tag=None):
+            codes = tile([P, P], U32, "val_codes%d" % t, tag)
+            scales = tile([P, P], U8, "val_scales%d" % t)
+            quantize(val_grouped[t][:], codes[:], scales[:])
+            return codes, scales
+
+        val_grouped = [pick_values(0, "bank_a")]
+        factor_rows = ps.tile([P, PACK, P], F32, tag="bank_a")
+        for r in range(PACK):
+            nc.tensor.transpose(factor_rows[:, r, :], factor_cols[:, r : r + 1].to_broadcast([P, P]), identity[:])
+
+        page_sum = tile([P, HALVES, PAGES], F32, "page_sum", "buffer0")
+        page_tanh = tile([P, HALVES, PAGES], F32, "page_tanh")
+        page_gain = tile([P, HALVES, PAGES], F32, "page_gain")
+        for h in halves:
+            nc.vector.tensor_reduce(page_sum[:, h, :], scores[h][:], AXIS.X, ALU.add)
+            nc.scalar.activation(page_tanh[:, h, :], page_sum[:, h, :], ACT.Tanh, scale=2.0 / PAGE)
+            nc.scalar.activation(
+                page_gain[:, h, :],
+                page_tanh[:, h, :],
+                ACT.Identity,
+                bias=half_help_1[:, h : h + 1],
+                scale=half_help[:, h : h + 1],
+            )
+        val_grouped.append(pick_values(1, "bank_b"))
+
+        helped = tile([P, HALVES, SLOTS], F32, "helped", "buffer1")
+        for h in halves:
+            nc.vector.tensor_tensor(
+                helped[:, h, :].rearrange("p (g k) -> p g k", k=PAGE),
+                scores[h][:],
+                page_gain[:, h, :].unsqueeze(2).to_broadcast([P, PAGES, PAGE]),
+                ALU.mult,
+            )
+        neg_max = [tile([P, 1], F32, "neg_max%d" % h) for h in halves]
+        row_sum = [tile([P, 1], F32, "row_sum%d" % h) for h in halves]
+        prob = [tile([P, SLOTS], F32, "prob%d" % h) for h in halves]
+        for h in halves:
+            nc.vector.tensor_reduce(neg_max[h][:], helped[:, h, :], AXIS.X, ALU.max, negate=True)
+            nc.scalar.activation(prob[h][:], helped[:, h, :], ACT.Exp, bias=neg_max[h][:], accum_out=row_sum[h][:])
+        val_mx = [quantize_values(0, "page_gain"), quantize_values(1)]
+        val_grouped.append(pick_values(2, "bank_b"))
+
+        inv_sum = tile([P, HALVES], F32, "inv_sum", "buffer2")
+        for h in halves:
+            nc.vector.reciprocal(inv_sum[:, h : h + 1], row_sum[h][:])
+        weight_grouped = []
+        for h in halves:
+            weight_bf = tile([P, SLOTS], BF16, "weight_bf%d" % h)
+            nc.vector.scalar_tensor_tensor(
+                weight_bf[:].rearrange("p (s r) -> p s r", r=PACK),
+                prob[h][:].rearrange("p (s r) -> p s r", r=PACK),
+                inv_sum[:, h : h + 1],
+                factor_rows[:].rearrange("p r s -> p s r"),
+                ALU.mult,
+                ALU.mult,
+            )
+            weight_grouped.append(turn_slots(weight_bf, "weight%d" % h, ("bank_c", "bank_d")[h]))
+        val_mx.append(quantize_values(2))
+        val_grouped.append(pick_values(3, "bank_b"))
+
+        weight_codes = tile([P, Q], U32, "weight_codes", "buffer3")
+        weight_scales = tile([P, Q], U8, "weight_scales")
+        for h in halves:
+            quantize(weight_grouped[h][:], weight_codes[:, cols[h]], weight_scales[:, cols[h]])
+
+        results = [ps.tile([P, PACK, P], F32, name="result%d" % h) for h in halves]
+
+        def multiply(t):
+            for h in halves:
+                nc.tensor.matmul_mx(
+                    out=results[h][:, t, :],
+                    lhsT=val_mx[t][0][:].bitcast(FP8X4),
+                    lhsT_scale=val_mx[t][1][:],
+                    rhs=weight_codes[:, cols[h]].bitcast(FP8X4),
+                    rhs_scale=weight_scales[:, cols[h]],
+                    start=True,
+                    stop=True,
+                )
+
+        out_rows = out_0.rearrange("(p t) q -> p t q", t=PACK)
+
+        def store_rows(first, last, queue):
+            staged = tile([P, last - first, Q], F32, "staged%d" % first)
+            for h in halves:
+                nc.scalar.copy(staged[:, :, cols[h]], results[h][:, first:last, :])
+            queue.dma_start(out_rows[:, first:last, :], staged[:])
+
+        for t in range(PACK - 1):
+            multiply(t)
+        store_rows(0, PACK - 1, nc.sync)
+        val_mx.append(quantize_values(PACK - 1))
+        multiply(PACK - 1)
+
+        result_bf = [tile([P, P, PACK], BF16, "result_bf%d" % h) for h in halves]
+        nc.vector.tensor_copy(result_bf[0][:], results[0][:].rearrange("p t q -> p q t"))
+        nc.scalar.copy(result_bf[1][:], results[1][:].rearrange("p t q -> p q t"))
+        out_codes = tile([P, Q], U32, "out_codes")
+        out_scales = tile([P, Q], U8, "out_scales")
+        for h in reversed(halves):
+            quantize(result_bf[h][:].rearrange("p q t -> p (q t)"), out_codes[:, cols[h]], out_scales[:, cols[h]])
+        store_rows(PACK - 1, PACK, nc.scalar)
+        nc.sync.dma_start(out_1[0].rearrange("p q r -> p (q r)").bitcast(I32), out_codes[:].bitcast(I32))
+        for quad in range(4):
+            queue = nc.scalar if quad % 2 else nc.sync
+            queue.dma_start(
+                out_2[0][4 * quad : 4 * quad + 4, :].bitcast(I32),
+                out_scales[32 * quad : 32 * quad + 4, :].bitcast(I32),
+            )

@@ -1,6 +1,7 @@
 from contextlib import ExitStack
 
 import concourse.mybir as mybir
+from concourse.masks import make_identity
 
 D, E, T, SLOTS, Q, PAGES = 512, 512, 2048, 512, 256, 32
 PAGE = SLOTS // PAGES
@@ -39,38 +40,38 @@ def tile_attend_pagemates_pl_kernel(
 
         key_scale_pool = tile([P, T], U8, "key_scale_pool", "buffer3")
         nc.vector.memset(key_scale_pool[:].bitcast(I32), 0)
-        zeros = tile([P, P], F32, "zeros", "columns")
-        nc.vector.memset(zeros[:], 0.0)
-        identity = tile([P, P], F32, "identity")
-        nc.gpsimd.affine_select(
-            out=identity[:],
-            in_=zeros[:],
-            compare_op=ALU.not_equal,
-            fill=1.0,
-            base=0,
-            pattern=[[-1, P]],
-            channel_multiplier=1,
-        )
 
         offsets = sb.tile([P, SLOTS // 16], U16)
         nc.sync.dma_start(offsets[:], offs)
-        help_cols = tile([P, HALVES], F32, "help_cols", "buffer0")
-        with nc.allow_non_contiguous_dma(reason="one help value a partition for each half of the query rows"):
-            nc.sync.dma_start(help_cols[:], helpf.rearrange("(h p) o -> p (h o)", p=P))
-        key_word_pool = tile([P, T], U16, "key_word_pool", "buffer1")
+        key_word_pool = tile([P, T], U16, "key_word_pool", "buffer2")
         nc.sync.dma_start(key_word_pool[:].bitcast(I32), keys_words[0].bitcast(I32))
-        query_raw = tile([P, PACK, Q], F32, "query_raw", "buffer2")
+        query_raw = tile([P, PACK, Q], F32, "query_raw")
         nc.sync.dma_start(query_raw[:], query.rearrange("(p j) q -> p j q", j=PACK))
         for quad in range(4):
             nc.scalar.dma_start(
                 key_scale_pool[32 * quad : 32 * quad + 4, :].bitcast(I32),
                 keys_scales[0][4 * quad : 4 * quad + 4, :].bitcast(I32),
             )
+        val_rows = vals.rearrange("(p t) c -> t p c", t=PACK)
 
+        def load_values(t):
+            val_pool = tile([P, T], F32, "val_pool%d" % t, "buffer%d" % t)
+            nc.sync.dma_start(val_pool[:], val_rows[t])
+            return val_pool
+
+        val_pools = [load_values(0), load_values(1)]
+
+        help_cols = tile([P, HALVES], F32, "help_cols")
+        with nc.allow_non_contiguous_dma(reason="one help value a partition for each half of the query rows"):
+            nc.gpsimd.dma_start(help_cols[:], helpf.rearrange("(h p) o -> p (h o)", p=P))
+        factor_cols = tile([P, PACK], F32, "factor_cols")
+        nc.gpsimd.dma_start(factor_cols[:], slot_factor.rearrange("o (s r) -> s (o r)", r=PACK))
+        identity = tile([P, P], F32, "identity")
+        make_identity(nc, identity[:])
         half_help = tile([P, HALVES], F32, "half_help")
-        nc.vector.tensor_scalar(half_help[:], help_cols[:], 0.5, None, ALU.mult)
+        nc.gpsimd.tensor_scalar(half_help[:], help_cols[:], 0.5, 0.0, ALU.mult, ALU.add)
         half_help_1 = tile([P, HALVES], F32, "half_help_1")
-        nc.vector.tensor_scalar(half_help_1[:], help_cols[:], 0.5, 1.0, ALU.mult, ALU.add)
+        nc.gpsimd.tensor_scalar(half_help_1[:], help_cols[:], 0.5, 1.0, ALU.mult, ALU.add)
 
         key_words = tile([P, SLOTS], U16, "key_words")
         nc.vector.tensor_copy(key_words[:], key_word_pool[:].indirect(offsets[:]))
@@ -87,17 +88,7 @@ def tile_attend_pagemates_pl_kernel(
             nc.scalar.activation(query_bf[:], query_raw[:, :, cols[h]].rearrange("p j q -> p q j"), ACT.Copy)
             quantize(query_bf[:].rearrange("p q j -> p (q j)"), query_codes[:, cols[h]], query_scales[:, cols[h]])
 
-        val_rows = vals.rearrange("(p t) c -> t p c", t=PACK)
-
-        def load_values(t):
-            val_pool = tile([P, T], F32, "val_pool%d" % t, "buffer%d" % t)
-            nc.sync.dma_start(val_pool[:], val_rows[t])
-            return val_pool
-
-        val_pools = [load_values(0)]
-        factor_cols = tile([P, PACK], F32, "factor_cols", "columns")
-        nc.sync.dma_start(factor_cols[:], slot_factor.rearrange("o (s r) -> s (o r)", r=PACK))
-        val_pools.extend([load_values(1), load_values(2)])
+        val_pools.append(load_values(2))
 
         scores = [ps.tile([P, PAGES, PAGE], F32, name="scores%d" % h) for h in halves]
         for h in halves:
@@ -112,30 +103,26 @@ def tile_attend_pagemates_pl_kernel(
             )
         val_pools.append(load_values(3))
 
-        def turn_slots(rows_bf, name, bank):
-            words = rows_bf[:].bitcast(F32)
-            turned = ps.tile([P, 2, P], F32, name=name + "_turned", tag=bank)
+        def turn_slots(word_halves, grouped, name, bank):
+            turned = ps.tile([P, 2, P], F32, name=name, tag=bank)
             for u in range(2):
-                nc.tensor.transpose(turned[:, u, :], words[:, u : SLOTS // 2 : 2], identity[:])
-            grouped = tile([P, P * PACK], BF16, name + "_grouped")
+                nc.tensor.transpose(turned[:, u, :], word_halves[u], identity[:])
             nc.scalar.copy(
-                grouped[:].bitcast(F32).rearrange("p (c u) -> p c u", u=2),
+                grouped.bitcast(F32).rearrange("p (c u) -> p c u", u=2),
                 turned[:].rearrange("p u c -> p c u"),
             )
-            return grouped
 
-        def pick_values(t, bank):
-            picked = tile([P, SLOTS], BF16, "picked%d" % t)
+        val_grouped = [tile([P, 2 * SLOTS], BF16, "val_grouped%d" % pair) for pair in range(PACK // 2)]
+
+        def pick_values(t, bank, tag=None):
+            picked = tile([P, SLOTS], BF16, "picked%d" % t, tag)
             nc.vector.tensor_copy(picked[:], val_pools[t][:].indirect(offsets[:]))
-            return turn_slots(picked, "val%d" % t, bank)
+            place = slice(t % 2 * SLOTS, (t % 2 + 1) * SLOTS)
+            words = picked[:].bitcast(F32)
+            word_halves = [words[:, u : SLOTS // 2 : 2] for u in range(2)]
+            turn_slots(word_halves, val_grouped[t // 2][:, place], "val_turned%d" % t, bank)
 
-        def quantize_values(t, tag=None):
-            codes = tile([P, P], U32, "val_codes%d" % t, tag)
-            scales = tile([P, P], U8, "val_scales%d" % t)
-            quantize(val_grouped[t][:], codes[:], scales[:])
-            return codes, scales
-
-        val_grouped = [pick_values(0, "bank_a")]
+        pick_values(0, "bank_a")
         factor_rows = ps.tile([P, PACK, P], F32, tag="bank_a")
         for r in range(PACK):
             nc.tensor.transpose(factor_rows[:, r, :], factor_cols[:, r : r + 1].to_broadcast([P, P]), identity[:])
@@ -153,7 +140,7 @@ def tile_attend_pagemates_pl_kernel(
                 bias=half_help_1[:, h : h + 1],
                 scale=half_help[:, h : h + 1],
             )
-        val_grouped.append(pick_values(1, "bank_b"))
+        pick_values(1, "bank_b", "picked0")
 
         helped = tile([P, HALVES, SLOTS], F32, "helped", "buffer1")
         for h in halves:
@@ -164,74 +151,73 @@ def tile_attend_pagemates_pl_kernel(
                 ALU.mult,
             )
         neg_max = [tile([P, 1], F32, "neg_max%d" % h) for h in halves]
-        row_sum = [tile([P, 1], F32, "row_sum%d" % h) for h in halves]
+        row_sum = tile([P, HALVES], F32, "row_sum")
         prob = [tile([P, SLOTS], F32, "prob%d" % h) for h in halves]
         for h in halves:
             nc.vector.tensor_reduce(neg_max[h][:], helped[:, h, :], AXIS.X, ALU.max, negate=True)
-            nc.scalar.activation(prob[h][:], helped[:, h, :], ACT.Exp, bias=neg_max[h][:], accum_out=row_sum[h][:])
-        val_mx = [quantize_values(0, "page_gain"), quantize_values(1)]
-        val_grouped.append(pick_values(2, "bank_b"))
-
-        inv_sum = tile([P, HALVES], F32, "inv_sum", "buffer2")
-        for h in halves:
-            nc.vector.reciprocal(inv_sum[:, h : h + 1], row_sum[h][:])
-        weight_grouped = []
-        for h in halves:
-            weight_bf = tile([P, SLOTS], BF16, "weight_bf%d" % h)
-            nc.vector.scalar_tensor_tensor(
-                weight_bf[:].rearrange("p (s r) -> p s r", r=PACK),
-                prob[h][:].rearrange("p (s r) -> p s r", r=PACK),
-                inv_sum[:, h : h + 1],
-                factor_rows[:].rearrange("p r s -> p s r"),
-                ALU.mult,
-                ALU.mult,
+            nc.scalar.activation(
+                prob[h][:], helped[:, h, :], ACT.Exp, bias=neg_max[h][:], accum_out=row_sum[:, h : h + 1]
             )
-            weight_grouped.append(turn_slots(weight_bf, "weight%d" % h, ("bank_c", "bank_d")[h]))
-        val_mx.append(quantize_values(2))
-        val_grouped.append(pick_values(3, "bank_b"))
+        pick_values(2, "bank_c", "page_gain")
+        inv_sum = tile([P, HALVES], F32, "inv_sum", "buffer2")
+        nc.vector.reciprocal(inv_sum[:], row_sum[:])
+        pick_values(3, "bank_b")
 
-        weight_codes = tile([P, Q], U32, "weight_codes", "buffer3")
-        weight_scales = tile([P, Q], U8, "weight_scales")
+        weight_grouped = [tile([P, SLOTS], BF16, "weight_grouped%d" % h) for h in halves]
         for h in halves:
-            quantize(weight_grouped[h][:], weight_codes[:, cols[h]], weight_scales[:, cols[h]])
-
-        results = [ps.tile([P, PACK, P], F32, name="result%d" % h) for h in halves]
-
-        def multiply(t):
-            for h in halves:
-                nc.tensor.matmul_mx(
-                    out=results[h][:, t, :],
-                    lhsT=val_mx[t][0][:].bitcast(FP8X4),
-                    lhsT_scale=val_mx[t][1][:],
-                    rhs=weight_codes[:, cols[h]].bitcast(FP8X4),
-                    rhs_scale=weight_scales[:, cols[h]],
-                    start=True,
-                    stop=True,
+            word_halves = []
+            for u in range(2):
+                pairs = slice(2 * u, 2 * u + 2)
+                weight_bf = tile([P, P, 2], BF16, "weight_bf%d_%d" % (h, u), "buffer3" if h + u == 0 else None)
+                nc.vector.scalar_tensor_tensor(
+                    weight_bf[:],
+                    prob[h][:].rearrange("p (s r) -> p s r", r=PACK)[:, :, pairs],
+                    inv_sum[:, h : h + 1],
+                    factor_rows[:, pairs, :].rearrange("p r s -> p s r"),
+                    ALU.mult,
+                    ALU.mult,
                 )
+                word_halves.append(weight_bf[:].rearrange("p s r -> p (s r)").bitcast(F32))
+            turn_slots(word_halves, weight_grouped[h][:], "weight_turned%d" % h, ("bank_d", "bank_c")[h])
+
+        val_codes = tile([P, E], U32, "val_codes", "prob1")
+        val_scales = tile([P, E], U8, "val_scales")
+        for pair in range(PACK // 2):
+            place = slice(pair * 2 * P, (pair + 1) * 2 * P)
+            quantize(val_grouped[pair][:], val_codes[:, place], val_scales[:, place])
 
         out_rows = out_0.rearrange("(p t) q -> p t q", t=PACK)
-
-        def store_rows(first, last, queue):
-            staged = tile([P, last - first, Q], F32, "staged%d" % first)
-            for h in halves:
-                nc.scalar.copy(staged[:, :, cols[h]], results[h][:, first:last, :])
-            queue.dma_start(out_rows[:, first:last, :], staged[:])
-
-        for t in range(PACK - 1):
-            multiply(t)
-        store_rows(0, PACK - 1, nc.sync)
-        val_mx.append(quantize_values(PACK - 1))
-        multiply(PACK - 1)
-
-        result_bf = [tile([P, P, PACK], BF16, "result_bf%d" % h) for h in halves]
-        nc.vector.tensor_copy(result_bf[0][:], results[0][:].rearrange("p t q -> p q t"))
-        nc.scalar.copy(result_bf[1][:], results[1][:].rearrange("p t q -> p q t"))
+        out_words = out_1[0].rearrange("p q r -> p (q r)").bitcast(I32)
         out_codes = tile([P, Q], U32, "out_codes")
         out_scales = tile([P, Q], U8, "out_scales")
-        for h in reversed(halves):
-            quantize(result_bf[h][:].rearrange("p q t -> p (q t)"), out_codes[:, cols[h]], out_scales[:, cols[h]])
-        store_rows(PACK - 1, PACK, nc.scalar)
-        nc.sync.dma_start(out_1[0].rearrange("p q r -> p (q r)").bitcast(I32), out_codes[:].bitcast(I32))
+        staged = [tile([P, PACK, P], F32, "staged%d" % h) for h in halves]
+        for h in halves:
+            weight_codes = tile([P, P], U32, "weight_codes%d" % h)
+            weight_scales = tile([P, P], U8, "weight_scales%d" % h)
+            quantize(weight_grouped[h][:], weight_codes[:], weight_scales[:])
+            for pair in range(PACK // 2):
+                bank = "scores%d" % h if pair == 0 else "result%d" % h
+                result = ps.tile([P, 2, P], F32, name="result%d_%d" % (h, pair), tag=bank)
+                for j in range(2):
+                    t = 2 * pair + j
+                    nc.tensor.matmul_mx(
+                        out=result[:, j, :],
+                        lhsT=val_codes[:, t * P : (t + 1) * P].bitcast(FP8X4),
+                        lhsT_scale=val_scales[:, t * P : (t + 1) * P],
+                        rhs=weight_codes[:].bitcast(FP8X4),
+                        rhs_scale=weight_scales[:],
+                        start=True,
+                        stop=True,
+                    )
+                copy = nc.vector.tensor_copy if (h, pair) == (0, 1) else nc.scalar.copy
+                copy(staged[h][:, 2 * pair : 2 * pair + 2, :], result[:])
+            nc.scalar.dma_start(out_rows[:, :, cols[h]], staged[h][:])
+
+        for h in halves:
+            result_bf = tile([P, P, PACK], BF16, "result_bf%d" % h)
+            nc.vector.tensor_copy(result_bf[:], staged[h][:].rearrange("p t q -> p q t"))
+            quantize(result_bf[:].rearrange("p q t -> p (q t)"), out_codes[:, cols[h]], out_scales[:, cols[h]])
+            nc.sync.dma_start(out_words[:, cols[h]], out_codes[:, cols[h]].bitcast(I32))
         for quad in range(4):
             queue = nc.scalar if quad % 2 else nc.sync
             queue.dma_start(

@@ -41,37 +41,28 @@ def tile_attend_pagemates_pl_kernel(
         key_scale_pool = tile([P, T], U8, "key_scale_pool", "buffer3")
         nc.vector.memset(key_scale_pool[:].bitcast(I32), 0)
 
+        identity = tile([P, P], F32, "identity")
+        make_identity(nc, identity[:])
+
         offsets = sb.tile([P, SLOTS // 16], U16)
         nc.sync.dma_start(offsets[:], offs)
-        key_word_pool = tile([P, T], U16, "key_word_pool", "buffer2")
+        help_cols = tile([P, HALVES], F32, "help_cols", "buffer0")
+        with nc.allow_non_contiguous_dma(reason="one help value a partition for each half of the query rows"):
+            nc.sync.dma_start(help_cols[:], helpf.rearrange("(h p) o -> p (h o)", p=P))
+        key_word_pool = tile([P, T], U16, "key_word_pool", "buffer1")
         nc.sync.dma_start(key_word_pool[:].bitcast(I32), keys_words[0].bitcast(I32))
-        query_raw = tile([P, PACK, Q], F32, "query_raw")
+        query_raw = tile([P, PACK, Q], F32, "query_raw", "buffer2")
         nc.sync.dma_start(query_raw[:], query.rearrange("(p j) q -> p j q", j=PACK))
         for quad in range(4):
             nc.scalar.dma_start(
                 key_scale_pool[32 * quad : 32 * quad + 4, :].bitcast(I32),
                 keys_scales[0][4 * quad : 4 * quad + 4, :].bitcast(I32),
             )
-        val_rows = vals.rearrange("(p t) c -> t p c", t=PACK)
 
-        def load_values(t):
-            val_pool = tile([P, T], F32, "val_pool%d" % t, "buffer%d" % t)
-            nc.sync.dma_start(val_pool[:], val_rows[t])
-            return val_pool
-
-        val_pools = [load_values(0), load_values(1)]
-
-        help_cols = tile([P, HALVES], F32, "help_cols")
-        with nc.allow_non_contiguous_dma(reason="one help value a partition for each half of the query rows"):
-            nc.gpsimd.dma_start(help_cols[:], helpf.rearrange("(h p) o -> p (h o)", p=P))
-        factor_cols = tile([P, PACK], F32, "factor_cols")
-        nc.gpsimd.dma_start(factor_cols[:], slot_factor.rearrange("o (s r) -> s (o r)", r=PACK))
-        identity = tile([P, P], F32, "identity")
-        make_identity(nc, identity[:])
         half_help = tile([P, HALVES], F32, "half_help")
-        nc.gpsimd.tensor_scalar(half_help[:], help_cols[:], 0.5, 0.0, ALU.mult, ALU.add)
+        nc.vector.tensor_scalar(half_help[:], help_cols[:], 0.5, None, ALU.mult)
         half_help_1 = tile([P, HALVES], F32, "half_help_1")
-        nc.gpsimd.tensor_scalar(half_help_1[:], help_cols[:], 0.5, 1.0, ALU.mult, ALU.add)
+        nc.vector.tensor_scalar(half_help_1[:], half_help[:], 1.0, None, ALU.add)
 
         key_words = tile([P, SLOTS], U16, "key_words")
         nc.vector.tensor_copy(key_words[:], key_word_pool[:].indirect(offsets[:]))
@@ -84,11 +75,20 @@ def tile_attend_pagemates_pl_kernel(
         query_codes = tile([P, Q], U32, "query_codes", "buffer3")
         query_scales = tile([P, Q], U8, "query_scales")
         for h in halves:
-            query_bf = tile([P, P, PACK], BF16, "query_bf%d" % h, "picked0" if h == 0 else None)
+            query_bf = tile([P, P, PACK], BF16, "query_bf%d" % h, (None, "factor_cols")[h])
             nc.scalar.activation(query_bf[:], query_raw[:, :, cols[h]].rearrange("p j q -> p q j"), ACT.Copy)
             quantize(query_bf[:].rearrange("p q j -> p (q j)"), query_codes[:, cols[h]], query_scales[:, cols[h]])
 
-        val_pools.append(load_values(2))
+        val_rows = vals.rearrange("(p t) c -> t p c", t=PACK)
+
+        def load_values(t):
+            val_pool = tile([P, T], F32, "val_pool%d" % t, "buffer%d" % t)
+            nc.sync.dma_start(val_pool[:], val_rows[t])
+            return val_pool
+
+        val_pools = [load_values(t) for t in range(PACK - 1)]
+        factor_cols = tile([P, PACK], F32, "factor_cols")
+        nc.sync.dma_start(factor_cols[:], slot_factor.rearrange("o (s r) -> s (o r)", r=PACK))
 
         scores = [ps.tile([P, PAGES, PAGE], F32, name="scores%d" % h) for h in halves]
         for h in halves:
@@ -112,27 +112,24 @@ def tile_attend_pagemates_pl_kernel(
                 turned[:].rearrange("p u c -> p c u"),
             )
 
-        val_grouped = [tile([P, 2 * SLOTS], BF16, "val_grouped%d" % pair) for pair in range(PACK // 2)]
-
-        def pick_values(t, bank, tag=None):
+        def pick_values(t, tag=None):
             picked = tile([P, SLOTS], BF16, "picked%d" % t, tag)
             nc.vector.tensor_copy(picked[:], val_pools[t][:].indirect(offsets[:]))
+            return picked
+
+        def turn_values(t, picked, bank):
             place = slice(t % 2 * SLOTS, (t % 2 + 1) * SLOTS)
             words = picked[:].bitcast(F32)
             word_halves = [words[:, u : SLOTS // 2 : 2] for u in range(2)]
             turn_slots(word_halves, val_grouped[t // 2][:, place], "val_turned%d" % t, bank)
 
-        pick_values(0, "bank_a")
-        factor_rows = ps.tile([P, PACK, P], F32, tag="bank_a")
-        for r in range(PACK):
-            nc.tensor.transpose(factor_rows[:, r, :], factor_cols[:, r : r + 1].to_broadcast([P, P]), identity[:])
 
-        page_sum = tile([P, HALVES, PAGES], F32, "page_sum", "buffer0")
         page_tanh = tile([P, HALVES, PAGES], F32, "page_tanh")
         page_gain = tile([P, HALVES, PAGES], F32, "page_gain")
         for h in halves:
-            nc.vector.tensor_reduce(page_sum[:, h, :], scores[h][:], AXIS.X, ALU.add)
-            nc.scalar.activation(page_tanh[:, h, :], page_sum[:, h, :], ACT.Tanh, scale=2.0 / PAGE)
+            page_sum = tile([P, PAGES], F32, "page_sum%d" % h)
+            nc.vector.tensor_reduce(page_sum[:], scores[h][:], AXIS.X, ALU.add)
+            nc.scalar.activation(page_tanh[:, h, :], page_sum[:], ACT.Tanh, scale=2.0 / PAGE)
             nc.scalar.activation(
                 page_gain[:, h, :],
                 page_tanh[:, h, :],
@@ -140,9 +137,13 @@ def tile_attend_pagemates_pl_kernel(
                 bias=half_help_1[:, h : h + 1],
                 scale=half_help[:, h : h + 1],
             )
-        pick_values(1, "bank_b", "picked0")
+        val_grouped = [tile([P, 2 * SLOTS], BF16, "val_grouped%d" % pair) for pair in range(PACK // 2)]
+        turn_values(0, pick_values(0, "page_sum0"), "bank_a")
+        factor_rows = ps.tile([P, PACK, P], F32, tag="bank_a")
+        for r in range(PACK):
+            nc.tensor.transpose(factor_rows[:, r, :], factor_cols[:, r : r + 1].to_broadcast([P, P]), identity[:])
 
-        helped = tile([P, HALVES, SLOTS], F32, "helped", "buffer1")
+        helped = tile([P, HALVES, SLOTS], F32, "helped", "buffer0")
         for h in halves:
             nc.vector.tensor_tensor(
                 helped[:, h, :].rearrange("p (g k) -> p g k", k=PAGE),
@@ -158,10 +159,11 @@ def tile_attend_pagemates_pl_kernel(
             nc.scalar.activation(
                 prob[h][:], helped[:, h, :], ACT.Exp, bias=neg_max[h][:], accum_out=row_sum[:, h : h + 1]
             )
-        pick_values(2, "bank_c", "page_gain")
-        inv_sum = tile([P, HALVES], F32, "inv_sum", "buffer2")
+        turn_values(1, pick_values(1, "page_gain"), "bank_b")
+        inv_sum = tile([P, HALVES], F32, "inv_sum", "buffer1")
         nc.vector.reciprocal(inv_sum[:], row_sum[:])
-        pick_values(3, "bank_b")
+        turn_values(2, pick_values(2), "bank_c")
+        turn_values(3, pick_values(3), "bank_b")
 
         weight_grouped = [tile([P, SLOTS], BF16, "weight_grouped%d" % h) for h in halves]
         for h in halves:

@@ -8,6 +8,12 @@ PAGE = SLOTS // PAGES
 P = 128
 PACK = 4
 HALVES = Q // P
+PAIRS = PACK // 2
+LIST_ROWS = 16
+QUADRANTS = 4
+QUADRANT = P // QUADRANTS
+SCALE_ROWS = 4
+SCALAR_SET = 3
 
 FLOPS = 2 * D * Q * SLOTS + 2 * SLOTS * E * Q
 
@@ -22,6 +28,14 @@ FP4X4 = mybir.dt.float4_e2m1fn_x4
 ALU = mybir.AluOpType
 ACT = mybir.ActivationFunctionType
 AXIS = mybir.AxisListType
+
+
+def scale_partitions(quadrant):
+    return slice(QUADRANT * quadrant, QUADRANT * quadrant + SCALE_ROWS)
+
+
+def scale_rows(quadrant):
+    return slice(SCALE_ROWS * quadrant, SCALE_ROWS * (quadrant + 1))
 
 
 def tile_attend_pagemates_pl_kernel(
@@ -44,7 +58,7 @@ def tile_attend_pagemates_pl_kernel(
         identity = tile([P, P], F32, "identity")
         make_identity(nc, identity[:])
 
-        offsets = sb.tile([P, SLOTS // 16], U16)
+        offsets = sb.tile([P, SLOTS // LIST_ROWS], U16)
         nc.sync.dma_start(offsets[:], offs)
         help_cols = tile([P, HALVES], F32, "help_cols", "buffer0")
         with nc.allow_non_contiguous_dma(reason="one help value a partition for each half of the query rows"):
@@ -53,10 +67,10 @@ def tile_attend_pagemates_pl_kernel(
         nc.sync.dma_start(key_word_pool[:].bitcast(I32), keys_words[0].bitcast(I32))
         query_raw = tile([P, PACK, Q], F32, "query_raw", "buffer2")
         nc.sync.dma_start(query_raw[:], query.rearrange("(p j) q -> p j q", j=PACK))
-        for quad in range(4):
+        for quadrant in range(QUADRANTS):
             nc.scalar.dma_start(
-                key_scale_pool[32 * quad : 32 * quad + 4, :].bitcast(I32),
-                keys_scales[0][4 * quad : 4 * quad + 4, :].bitcast(I32),
+                key_scale_pool[scale_partitions(quadrant), :].bitcast(I32),
+                keys_scales[0][scale_rows(quadrant), :].bitcast(I32),
             )
 
         half_help = tile([P, HALVES], F32, "half_help")
@@ -80,13 +94,15 @@ def tile_attend_pagemates_pl_kernel(
             quantize(query_bf[:].rearrange("p q j -> p (q j)"), query_codes[:, cols[h]], query_scales[:, cols[h]])
 
         val_rows = vals.rearrange("(p t) c -> t p c", t=PACK)
+        val_pools = {}
 
-        def load_values(t):
-            val_pool = tile([P, T], F32, "val_pool%d" % t, "buffer%d" % t)
-            nc.sync.dma_start(val_pool[:], val_rows[t])
-            return val_pool
+        def load_values(t, tag):
+            val_pools[t] = tile([P, T], F32, "val_pool%d" % t, tag)
+            nc.sync.dma_start(val_pools[t][:], val_rows[t])
 
-        val_pools = [load_values(t) for t in range(PACK - 1)]
+        load_values(0, "buffer0")
+        load_values(SCALAR_SET, "buffer1")
+        load_values(1, "buffer2")
         factor_cols = tile([P, PACK], F32, "factor_cols")
         nc.sync.dma_start(factor_cols[:], slot_factor.rearrange("o (s r) -> s (o r)", r=PACK))
 
@@ -101,14 +117,14 @@ def tile_attend_pagemates_pl_kernel(
                 start=True,
                 stop=True,
             )
-        val_pools.append(load_values(3))
+        load_values(2, "buffer3")
 
-        def turn_slots(word_halves, grouped, name, bank):
-            turned = ps.tile([P, 2, P], F32, name=name, tag=bank)
-            for u in range(2):
-                nc.tensor.transpose(turned[:, u, :], word_halves[u], identity[:])
+        def turn_slots(words_by_pair, grouped, name, bank):
+            turned = ps.tile([P, PAIRS, P], F32, name=name, tag=bank)
+            for u in range(PAIRS):
+                nc.tensor.transpose(turned[:, u, :], words_by_pair[u], identity[:])
             nc.scalar.copy(
-                grouped.bitcast(F32).rearrange("p (c u) -> p c u", u=2),
+                grouped.bitcast(F32).rearrange("p (c u) -> p c u", u=PAIRS),
                 turned[:].rearrange("p u c -> p c u"),
             )
 
@@ -120,9 +136,8 @@ def tile_attend_pagemates_pl_kernel(
         def turn_values(t, picked, bank):
             place = slice(t % 2 * SLOTS, (t % 2 + 1) * SLOTS)
             words = picked[:].bitcast(F32)
-            word_halves = [words[:, u : SLOTS // 2 : 2] for u in range(2)]
-            turn_slots(word_halves, val_grouped[t // 2][:, place], "val_turned%d" % t, bank)
-
+            words_by_pair = [words[:, u : SLOTS // 2 : PAIRS] for u in range(PAIRS)]
+            turn_slots(words_by_pair, val_grouped[t // 2][:, place], "val_turned%d" % t, bank)
 
         page_tanh = tile([P, HALVES, PAGES], F32, "page_tanh")
         page_gain = tile([P, HALVES, PAGES], F32, "page_gain")
@@ -137,8 +152,10 @@ def tile_attend_pagemates_pl_kernel(
                 bias=half_help_1[:, h : h + 1],
                 scale=half_help[:, h : h + 1],
             )
-        val_grouped = [tile([P, 2 * SLOTS], BF16, "val_grouped%d" % pair) for pair in range(PACK // 2)]
+
+        val_grouped = [tile([P, 2 * SLOTS], BF16, "val_grouped%d" % pair) for pair in range(PAIRS)]
         turn_values(0, pick_values(0, "page_sum0"), "bank_a")
+
         factor_rows = ps.tile([P, PACK, P], F32, tag="bank_a")
         for r in range(PACK):
             nc.tensor.transpose(factor_rows[:, r, :], factor_cols[:, r : r + 1].to_broadcast([P, P]), identity[:])
@@ -151,40 +168,47 @@ def tile_attend_pagemates_pl_kernel(
                 page_gain[:, h, :].unsqueeze(2).to_broadcast([P, PAGES, PAGE]),
                 ALU.mult,
             )
+
+        val_pool_bf = tile([P, T], BF16, "val_pool_bf")
+        nc.scalar.activation(val_pool_bf[:], val_pools[SCALAR_SET][:], ACT.Copy)
         neg_max = [tile([P, 1], F32, "neg_max%d" % h) for h in halves]
         row_sum = tile([P, HALVES], F32, "row_sum")
-        prob = [tile([P, SLOTS], F32, "prob%d" % h) for h in halves]
+        prob = tile([P, HALVES, SLOTS], F32, "prob", "buffer1")
         for h in halves:
             nc.vector.tensor_reduce(neg_max[h][:], helped[:, h, :], AXIS.X, ALU.max, negate=True)
             nc.scalar.activation(
-                prob[h][:], helped[:, h, :], ACT.Exp, bias=neg_max[h][:], accum_out=row_sum[:, h : h + 1]
+                prob[:, h, :], helped[:, h, :], ACT.Exp, bias=neg_max[h][:], accum_out=row_sum[:, h : h + 1]
             )
+
         turn_values(1, pick_values(1, "page_gain"), "bank_b")
-        inv_sum = tile([P, HALVES], F32, "inv_sum", "buffer1")
+        inv_sum = tile([P, HALVES], F32, "inv_sum", "buffer2")
         nc.vector.reciprocal(inv_sum[:], row_sum[:])
+        scalar_picked = tile([P, SLOTS], BF16, "picked%d" % SCALAR_SET)
+        nc.scalar.activation(scalar_picked[:], val_pool_bf[:].indirect(offsets[:]), ACT.Copy)
+        turn_values(SCALAR_SET, scalar_picked, "bank_d")
         turn_values(2, pick_values(2), "bank_c")
-        turn_values(3, pick_values(3), "bank_b")
 
         weight_grouped = [tile([P, SLOTS], BF16, "weight_grouped%d" % h) for h in halves]
         for h in halves:
-            word_halves = []
-            for u in range(2):
-                pairs = slice(2 * u, 2 * u + 2)
-                weight_bf = tile([P, P, 2], BF16, "weight_bf%d_%d" % (h, u), "buffer3" if h + u == 0 else None)
+            words_by_pair = []
+            for u in range(PAIRS):
+                places = slice(2 * u, 2 * u + 2)
+                first_weights = (h, u) == (0, 0)
+                weight_bf = tile([P, P, 2], BF16, "weight_bf%d_%d" % (h, u), "buffer3" if first_weights else None)
                 nc.vector.scalar_tensor_tensor(
                     weight_bf[:],
-                    prob[h][:].rearrange("p (s r) -> p s r", r=PACK)[:, :, pairs],
+                    prob[:, h, :].rearrange("p (s r) -> p s r", r=PACK)[:, :, places],
                     inv_sum[:, h : h + 1],
-                    factor_rows[:, pairs, :].rearrange("p r s -> p s r"),
+                    factor_rows[:, places, :].rearrange("p r s -> p s r"),
                     ALU.mult,
                     ALU.mult,
                 )
-                word_halves.append(weight_bf[:].rearrange("p s r -> p (s r)").bitcast(F32))
-            turn_slots(word_halves, weight_grouped[h][:], "weight_turned%d" % h, ("bank_d", "bank_c")[h])
+                words_by_pair.append(weight_bf[:].rearrange("p s r -> p (s r)").bitcast(F32))
+            turn_slots(words_by_pair, weight_grouped[h][:], "weight_turned%d" % h, ("bank_b", "bank_d")[h])
 
-        val_codes = tile([P, E], U32, "val_codes", "prob1")
+        val_codes = tile([P, E], U32, "val_codes", "buffer1")
         val_scales = tile([P, E], U8, "val_scales")
-        for pair in range(PACK // 2):
+        for pair in range(PAIRS):
             place = slice(pair * 2 * P, (pair + 1) * 2 * P)
             quantize(val_grouped[pair][:], val_codes[:, place], val_scales[:, place])
 
@@ -197,8 +221,8 @@ def tile_attend_pagemates_pl_kernel(
             weight_codes = tile([P, P], U32, "weight_codes%d" % h)
             weight_scales = tile([P, P], U8, "weight_scales%d" % h)
             quantize(weight_grouped[h][:], weight_codes[:], weight_scales[:])
-            for pair in range(PACK // 2):
-                bank = "scores%d" % h if pair == 0 else "result%d" % h
+            for pair in range(PAIRS):
+                bank = ("scores%d" % h, "result%d" % h)[pair]
                 result = ps.tile([P, 2, P], F32, name="result%d_%d" % (h, pair), tag=bank)
                 for j in range(2):
                     t = 2 * pair + j
@@ -211,7 +235,8 @@ def tile_attend_pagemates_pl_kernel(
                         start=True,
                         stop=True,
                     )
-                copy = nc.vector.tensor_copy if (h, pair) == (0, 1) else nc.scalar.copy
+                on_vector = (h, pair) == (0, 1)
+                copy = nc.vector.tensor_copy if on_vector else nc.scalar.copy
                 copy(staged[h][:, 2 * pair : 2 * pair + 2, :], result[:])
             nc.scalar.dma_start(out_rows[:, :, cols[h]], staged[h][:])
 
@@ -220,9 +245,9 @@ def tile_attend_pagemates_pl_kernel(
             nc.vector.tensor_copy(result_bf[:], staged[h][:].rearrange("p t q -> p q t"))
             quantize(result_bf[:].rearrange("p q t -> p (q t)"), out_codes[:, cols[h]], out_scales[:, cols[h]])
             nc.sync.dma_start(out_words[:, cols[h]], out_codes[:, cols[h]].bitcast(I32))
-        for quad in range(4):
-            queue = nc.scalar if quad % 2 else nc.sync
+        for quadrant in range(QUADRANTS):
+            queue = (nc.sync, nc.scalar)[quadrant % 2]
             queue.dma_start(
-                out_2[0][4 * quad : 4 * quad + 4, :].bitcast(I32),
-                out_scales[32 * quad : 32 * quad + 4, :].bitcast(I32),
+                out_2[0][scale_rows(quadrant), :].bitcast(I32),
+                out_scales[scale_partitions(quadrant), :].bitcast(I32),
             )

from contextlib import ExitStack

import concourse.mybir as mybir
from concourse.masks import make_identity

D, E, T, SLOTS, Q, PAGES = 512, 512, 2048, 512, 256, 32
PAGE = SLOTS // PAGES
P = 128
PACK = 4
HALVES = Q // P
PAIRS = PACK // 2
LIST_ROWS = 16
QUADRANTS = 4
QUADRANT = P // QUADRANTS
SCALE_ROWS = 4
SCALAR_SET = 3

FLOPS = 2 * D * Q * SLOTS + 2 * SLOTS * E * Q

F32 = mybir.dt.float32
BF16 = mybir.dt.bfloat16
I32 = mybir.dt.int32
U32 = mybir.dt.uint32
U16 = mybir.dt.uint16
U8 = mybir.dt.uint8
FP8X4 = mybir.dt.float8_e4m3fn_x4
FP4X4 = mybir.dt.float4_e2m1fn_x4
ALU = mybir.AluOpType
ACT = mybir.ActivationFunctionType
AXIS = mybir.AxisListType


def scale_partitions(quadrant):
    return slice(QUADRANT * quadrant, QUADRANT * quadrant + SCALE_ROWS)


def scale_rows(quadrant):
    return slice(SCALE_ROWS * quadrant, SCALE_ROWS * (quadrant + 1))


def tile_attend_pagemates_pl_kernel(
    tc, query, keys_words, keys_scales, helpf, slot_factor, vals, offs, out_0, out_1, out_2
):
    nc = tc.nc
    with ExitStack() as ctx:
        sb = ctx.enter_context(tc.tile_pool(name="sb", bufs=1))
        ps = ctx.enter_context(tc.psum_pool(name="ps", bufs=1))

        def tile(shape, dtype, name, tag=None):
            return sb.tile(shape, dtype, align_bytes=64, name=name, tag=tag or name)

        halves = range(HALVES)
        cols = [slice(h * P, (h + 1) * P) for h in halves]

        key_scale_pool = tile([P, T], U8, "key_scale_pool", "buffer3")
        nc.vector.memset(key_scale_pool[:].bitcast(I32), 0)

        identity = tile([P, P], F32, "identity")
        make_identity(nc, identity[:])

        offsets = sb.tile([P, SLOTS // LIST_ROWS], U16)
        nc.sync.dma_start(offsets[:], offs)
        help_cols = tile([P, HALVES], F32, "help_cols", "buffer0")
        with nc.allow_non_contiguous_dma(reason="one help value a partition for each half of the query rows"):
            nc.sync.dma_start(help_cols[:], helpf.rearrange("(h p) o -> p (h o)", p=P))
        key_word_pool = tile([P, T], U16, "key_word_pool", "buffer1")
        nc.sync.dma_start(key_word_pool[:].bitcast(I32), keys_words[0].bitcast(I32))
        query_raw = tile([P, PACK, Q], F32, "query_raw", "buffer2")
        nc.sync.dma_start(query_raw[:], query.rearrange("(p j) q -> p j q", j=PACK))
        for quadrant in range(QUADRANTS):
            nc.scalar.dma_start(
                key_scale_pool[scale_partitions(quadrant), :].bitcast(I32),
                keys_scales[0][scale_rows(quadrant), :].bitcast(I32),
            )

        half_help = tile([P, HALVES], F32, "half_help")
        nc.vector.tensor_scalar(half_help[:], help_cols[:], 0.5, None, ALU.mult)
        half_help_1 = tile([P, HALVES], F32, "half_help_1")
        nc.vector.tensor_scalar(half_help_1[:], half_help[:], 1.0, None, ALU.add)

        key_words = tile([P, SLOTS], U16, "key_words")
        nc.vector.tensor_copy(key_words[:], key_word_pool[:].indirect(offsets[:]))
        key_scales = tile([P, SLOTS], U8, "key_scales")
        nc.vector.tensor_copy(key_scales[:], key_scale_pool[:].indirect(offsets[:]))

        def quantize(grouped, codes, scales):
            nc.vector.quantize_mx(out=codes.bitcast(FP8X4), scales=scales, in_=grouped)

        query_codes = tile([P, Q], U32, "query_codes", "buffer3")
        query_scales = tile([P, Q], U8, "query_scales")
        for h in halves:
            query_bf = tile([P, P, PACK], BF16, "query_bf%d" % h, (None, "factor_cols")[h])
            nc.scalar.activation(query_bf[:], query_raw[:, :, cols[h]].rearrange("p j q -> p q j"), ACT.Copy)
            quantize(query_bf[:].rearrange("p q j -> p (q j)"), query_codes[:, cols[h]], query_scales[:, cols[h]])

        val_rows = vals.rearrange("(p t) c -> t p c", t=PACK)
        val_pools = {}

        def load_values(t, tag):
            val_pools[t] = tile([P, T], F32, "val_pool%d" % t, tag)
            nc.sync.dma_start(val_pools[t][:], val_rows[t])

        load_values(0, "buffer0")
        load_values(SCALAR_SET, "buffer1")
        load_values(1, "buffer2")
        factor_cols = tile([P, PACK], F32, "factor_cols")
        nc.sync.dma_start(factor_cols[:], slot_factor.rearrange("o (s r) -> s (o r)", r=PACK))

        scores = [ps.tile([P, PAGES, PAGE], F32, name="scores%d" % h) for h in halves]
        for h in halves:
            nc.tensor.matmul_mx(
                out=scores[h][:].rearrange("p g k -> p (g k)"),
                lhsT=query_codes[:, cols[h]].bitcast(FP8X4),
                lhsT_scale=query_scales[:, cols[h]],
                rhs=key_words[:].bitcast(FP4X4),
                rhs_scale=key_scales[:],
                start=True,
                stop=True,
            )
        load_values(2, "buffer3")

        def turn_slots(words_by_pair, grouped, name, bank):
            turned = ps.tile([P, PAIRS, P], F32, name=name, tag=bank)
            for u in range(PAIRS):
                nc.tensor.transpose(turned[:, u, :], words_by_pair[u], identity[:])
            nc.scalar.copy(
                grouped.bitcast(F32).rearrange("p (c u) -> p c u", u=PAIRS),
                turned[:].rearrange("p u c -> p c u"),
            )

        def pick_values(t, tag=None):
            picked = tile([P, SLOTS], BF16, "picked%d" % t, tag)
            nc.vector.tensor_copy(picked[:], val_pools[t][:].indirect(offsets[:]))
            return picked

        def turn_values(t, picked, bank):
            place = slice(t % 2 * SLOTS, (t % 2 + 1) * SLOTS)
            words = picked[:].bitcast(F32)
            words_by_pair = [words[:, u : SLOTS // 2 : PAIRS] for u in range(PAIRS)]
            turn_slots(words_by_pair, val_grouped[t // 2][:, place], "val_turned%d" % t, bank)

        page_tanh = tile([P, HALVES, PAGES], F32, "page_tanh")
        page_gain = tile([P, HALVES, PAGES], F32, "page_gain")
        for h in halves:
            page_sum = tile([P, PAGES], F32, "page_sum%d" % h)
            nc.vector.tensor_reduce(page_sum[:], scores[h][:], AXIS.X, ALU.add)
            nc.scalar.activation(page_tanh[:, h, :], page_sum[:], ACT.Tanh, scale=2.0 / PAGE)
            nc.scalar.activation(
                page_gain[:, h, :],
                page_tanh[:, h, :],
                ACT.Identity,
                bias=half_help_1[:, h : h + 1],
                scale=half_help[:, h : h + 1],
            )

        val_grouped = [tile([P, 2 * SLOTS], BF16, "val_grouped%d" % pair) for pair in range(PAIRS)]
        turn_values(0, pick_values(0, "page_sum0"), "bank_a")

        factor_rows = ps.tile([P, PACK, P], F32, tag="bank_a")
        for r in range(PACK):
            nc.tensor.transpose(factor_rows[:, r, :], factor_cols[:, r : r + 1].to_broadcast([P, P]), identity[:])

        helped = tile([P, HALVES, SLOTS], F32, "helped", "buffer0")
        for h in halves:
            nc.vector.tensor_tensor(
                helped[:, h, :].rearrange("p (g k) -> p g k", k=PAGE),
                scores[h][:],
                page_gain[:, h, :].unsqueeze(2).to_broadcast([P, PAGES, PAGE]),
                ALU.mult,
            )

        val_pool_bf = tile([P, T], BF16, "val_pool_bf")
        nc.scalar.activation(val_pool_bf[:], val_pools[SCALAR_SET][:], ACT.Copy)
        neg_max = [tile([P, 1], F32, "neg_max%d" % h) for h in halves]
        row_sum = tile([P, HALVES], F32, "row_sum")
        prob = tile([P, HALVES, SLOTS], F32, "prob", "buffer1")
        for h in halves:
            nc.vector.tensor_reduce(neg_max[h][:], helped[:, h, :], AXIS.X, ALU.max, negate=True)
            nc.scalar.activation(
                prob[:, h, :], helped[:, h, :], ACT.Exp, bias=neg_max[h][:], accum_out=row_sum[:, h : h + 1]
            )

        turn_values(1, pick_values(1, "page_gain"), "bank_b")
        inv_sum = tile([P, HALVES], F32, "inv_sum", "buffer2")
        nc.vector.reciprocal(inv_sum[:], row_sum[:])
        scalar_picked = tile([P, SLOTS], BF16, "picked%d" % SCALAR_SET)
        nc.scalar.activation(scalar_picked[:], val_pool_bf[:].indirect(offsets[:]), ACT.Copy)
        turn_values(SCALAR_SET, scalar_picked, "bank_d")
        turn_values(2, pick_values(2), "bank_c")

        weight_grouped = [tile([P, SLOTS], BF16, "weight_grouped%d" % h) for h in halves]
        for h in halves:
            words_by_pair = []
            for u in range(PAIRS):
                places = slice(2 * u, 2 * u + 2)
                first_weights = (h, u) == (0, 0)
                weight_bf = tile([P, P, 2], BF16, "weight_bf%d_%d" % (h, u), "buffer3" if first_weights else None)
                nc.vector.scalar_tensor_tensor(
                    weight_bf[:],
                    prob[:, h, :].rearrange("p (s r) -> p s r", r=PACK)[:, :, places],
                    inv_sum[:, h : h + 1],
                    factor_rows[:, places, :].rearrange("p r s -> p s r"),
                    ALU.mult,
                    ALU.mult,
                )
                words_by_pair.append(weight_bf[:].rearrange("p s r -> p (s r)").bitcast(F32))
            turn_slots(words_by_pair, weight_grouped[h][:], "weight_turned%d" % h, ("bank_b", "bank_d")[h])

        val_codes = tile([P, E], U32, "val_codes", "buffer1")
        val_scales = tile([P, E], U8, "val_scales")
        for pair in range(PAIRS):
            place = slice(pair * 2 * P, (pair + 1) * 2 * P)
            quantize(val_grouped[pair][:], val_codes[:, place], val_scales[:, place])

        out_rows = out_0.rearrange("(p t) q -> p t q", t=PACK)
        out_words = out_1[0].rearrange("p q r -> p (q r)").bitcast(I32)
        out_codes = tile([P, Q], U32, "out_codes")
        out_scales = tile([P, Q], U8, "out_scales")
        staged = [tile([P, PACK, P], F32, "staged%d" % h) for h in halves]
        for h in halves:
            weight_codes = tile([P, P], U32, "weight_codes%d" % h)
            weight_scales = tile([P, P], U8, "weight_scales%d" % h)
            quantize(weight_grouped[h][:], weight_codes[:], weight_scales[:])
            for pair in range(PAIRS):
                bank = ("scores%d" % h, "result%d" % h)[pair]
                result = ps.tile([P, 2, P], F32, name="result%d_%d" % (h, pair), tag=bank)
                for j in range(2):
                    t = 2 * pair + j
                    nc.tensor.matmul_mx(
                        out=result[:, j, :],
                        lhsT=val_codes[:, t * P : (t + 1) * P].bitcast(FP8X4),
                        lhsT_scale=val_scales[:, t * P : (t + 1) * P],
                        rhs=weight_codes[:].bitcast(FP8X4),
                        rhs_scale=weight_scales[:],
                        start=True,
                        stop=True,
                    )
                on_vector = (h, pair) == (0, 1)
                copy = nc.vector.tensor_copy if on_vector else nc.scalar.copy
                copy(staged[h][:, 2 * pair : 2 * pair + 2, :], result[:])
            nc.scalar.dma_start(out_rows[:, :, cols[h]], staged[h][:])

        for h in halves:
            result_bf = tile([P, P, PACK], BF16, "result_bf%d" % h)
            nc.vector.tensor_copy(result_bf[:], staged[h][:].rearrange("p t q -> p q t"))
            quantize(result_bf[:].rearrange("p q t -> p (q t)"), out_codes[:, cols[h]], out_scales[:, cols[h]])
            nc.sync.dma_start(out_words[:, cols[h]], out_codes[:, cols[h]].bitcast(I32))
        for quadrant in range(QUADRANTS):
            queue = (nc.sync, nc.scalar)[quadrant % 2]
            queue.dma_start(
                out_2[0][scale_rows(quadrant), :].bitcast(I32),
                out_scales[scale_partitions(quadrant), :].bitcast(I32),
            )
